import numpy as np
import ml_dtypes


def mxq(x, axis, fmt="e4m3"):
    dtype, down = {"e4m3": (ml_dtypes.float8_e4m3fn, 7), "e5m2": (ml_dtypes.float8_e5m2, 14)}[fmt]
    v = np.moveaxis(np.asarray(x, np.float32).astype(ml_dtypes.bfloat16).astype(np.float64), axis, -1)
    blocks = v.reshape(v.shape[:-1] + (-1, 32))
    amax = np.abs(blocks).max(-1, keepdims=True)
    byte = np.maximum(np.where(amax > 0, np.frexp(amax)[1] - 1 + 127, 0) - down, 1)
    scale = np.exp2(byte - 127.0)
    codes = (blocks / scale).astype(np.float32).astype(dtype).astype(np.float64)
    return np.moveaxis((codes * scale).reshape(v.shape), -1, axis)


WIDE = False


def mx_kscale(k):
    if not WIDE:
        return np.ones(k)
    levels = np.array([10, -10, 5, -5, 0])
    if k % 512:
        return np.exp2(np.random.permutation(np.resize(levels, k // 32))).repeat(32)
    a = np.empty((k // 512, 16))
    for p in range(k // 512):
        a[p, :8] = np.random.permutation(np.resize(levels, 8))
        for g in range(8):
            far = levels[np.abs(levels - a[p, g]) >= 10]
            a[p, g + 8] = far[np.random.randint(len(far))]
    return np.exp2(a.ravel()).repeat(32)


BF16 = ml_dtypes.bfloat16


def bf(x):
    return np.asarray(x, np.float32).astype(BF16)


def f64(x):
    return np.asarray(x).astype(np.float64)


E2M1 = np.array([0.0, 0.5, 1.0, 1.5, 2.0, 3.0, 4.0, 6.0, -0.0, -0.5, -1.0, -1.5, -2.0, -3.0, -4.0, -6.0])


def pack_weight(w, fmt):
    k, n = w.shape
    w = f64(bf(w)).reshape(k // 32, 32, n)
    amax = np.abs(w).max(1)
    if fmt == "e4m3":
        byte = np.frexp(amax)[1] - 1 + 127 - 7
    else:
        mant, ex = np.frexp(amax / 6.0)
        byte = np.where(mant > 0.5, ex, ex - 1) + 127
    byte = np.clip(np.where(amax > 0, byte, 1), 1, 254)
    scaled = (w * np.exp2(127.0 - byte)[:, None, :]).reshape(k, n).astype(np.float32)
    by_word = np.ascontiguousarray(scaled.reshape(k // 512, 128, 4, n).transpose(0, 1, 3, 2))
    if fmt == "e4m3":
        words = by_word.astype(ml_dtypes.float8_e4m3fn).view(np.uint8)
    else:
        c = by_word.astype(ml_dtypes.float4_e2m1fn).view(np.uint8) & 0xF
        words = c[..., 0::2] | (c[..., 1::2] << 4)
    return np.ascontiguousarray(words), np.ascontiguousarray(byte.astype(np.uint8).reshape(k // 512, 16, n))


def unpack_weight(words, scales, fmt):
    g, p, n, _ = words.shape
    if fmt == "e4m3":
        vals = np.ascontiguousarray(words).view(ml_dtypes.float8_e4m3fn).astype(np.float64)
    else:
        nib = np.empty((g, p, n, 4), np.uint8)
        nib[..., 0::2] = words & 0xF
        nib[..., 1::2] = words >> 4
        vals = E2M1[nib]
    vals = vals * np.repeat(np.exp2(scales.astype(np.float64) - 127.0), 8, axis=1)[..., None]
    return vals.transpose(0, 1, 3, 2).reshape(g * 512, n)
def pack4(w):
    words, scales = pack_weight(w, "e2m1")
    return words.reshape(words.shape[0], 128, -1), scales


def unpack4(words, scales):
    return unpack_weight(words.reshape(words.shape[0], 128, -1, 2), scales, "e2m1")


def planes(Y):
    n, m = Y.shape
    b = f64(bf(Y)).reshape(n // 32, 32, m)
    amax = np.abs(b).max(1)
    byte = np.clip(np.where(amax > 0, np.frexp(amax)[1] - 1 + 127 - 7, 1), 1, 254)
    codes = (b * np.exp2(127.0 - byte)[:, None, :]).reshape(n, m).astype(np.float32).astype(ml_dtypes.float8_e4m3fn).view(np.uint8)
    words = codes.reshape(n // 512, 128, 4, m).transpose(0, 1, 3, 2)
    return np.ascontiguousarray(words), np.ascontiguousarray(byte.astype(np.uint8).reshape(n // 512, 16, m))


B, H, C = 512, 512, 8
HC = C * H


def setup_inputs():
    s = mx_kscale(H)
    z0 = bf(np.random.standard_normal((B, H)))
    g = bf((1.0 + 0.1 * np.random.standard_normal(H)) * s)
    w_words, w_scales = pack4(np.random.standard_normal((H, HC)) / np.sqrt(H) / s[:, None])
    return {"z0": z0,
            "g": g,
            "w_words": w_words,
            "w_scales": w_scales,
            "dx0": bf(np.random.standard_normal((B, C)) * np.sqrt(2.0 / C)),
            "dxm": bf(np.random.standard_normal((B, C)) * np.sqrt(2.0 / C))}


def vector_field(z, g, wq, channels):
    batch, hidden = z.shape
    u = z * g[None, :]
    f = np.tanh(mxq(u, 1, "e4m3") @ wq)
    return f.reshape(batch, channels, hidden)


def apply_control(f, dx):
    return np.sum(f * dx[:, :, None], axis=1)


def core(z0, g, w_words, w_scales, dx0, dxm):
    z0, g, dx0, dxm = f64(z0), f64(g), f64(dx0), f64(dxm)
    channels = dx0.shape[1]
    wq = unpack4(w_words, w_scales)
    f0 = vector_field(z0, g, wq, channels)
    zmid = z0 + apply_control(f0, dx0)
    f1 = vector_field(zmid, g, wq, channels)
    return apply_control(f1, dxm)


def reference(z0, g, w_words, w_scales, dx0, dxm):
    R_out = core(z0, g, w_words, w_scales, dx0, dxm)
    words, scales = planes(R_out.T)
    return R_out, words, scales

from contextlib import ExitStack

import concourse.mybir as mybir
from concourse.masks import make_identity

B, H, C = 512, 512, 8
FLOPS = 2 * 2 * B * H * C * H

F32 = mybir.dt.float32
BF16 = mybir.dt.bfloat16
I32 = mybir.dt.int32
U32 = mybir.dt.uint32
U8 = mybir.dt.uint8
FP8X4 = mybir.dt.float8_e4m3fn_x4
FP4X4 = mybir.dt.float4_e2m1fn_x4
TANH = mybir.ActivationFunctionType.Tanh
MULT = mybir.AluOpType.mult
ADD = mybir.AluOpType.add

P = 128
TILES = B // P
HALF = H // 2
AHEAD = 4
JOBS = [(1, 0), (1, 1), (2, 0), (1, 2), (2, 1), (1, 3), (2, 2), (2, 3)]
W_GROUPS = [(0, 1), (1, 4), (4, 8)]
UNITS = len(JOBS) * C


def tile_neuralcdemidpointstep_x2_kernel(tc, z0, g, w_words, w_scales, dx0, dxm, out_0, out_1, out_2):
    nc = tc.nc
    with ExitStack() as ctx:
        keep = ctx.enter_context(tc.tile_pool(name="keep", bufs=1))
        flow = ctx.enter_context(tc.tile_pool(name="flow", bufs=6))
        stage = ctx.enter_context(tc.tile_pool(name="stage", bufs=2))
        mx_psum = ctx.enter_context(tc.psum_pool(name="mx_psum", bufs=AHEAD + 1))
        tr_psum = ctx.enter_context(tc.psum_pool(name="tr_psum", bufs=3))
        ctx.enter_context(tc.manual_schedule())

        ident = keep.tile([P, P], F32)
        gain = keep.tile([P, 4], BF16)
        w_plane = keep.tile([P, C * H], U8, align_bytes=64)
        z_sb = [keep.tile([P, H], BF16, name="z%d" % i) for i in range(TILES)]
        w_sb = [keep.tile([P, 2 * H * (hi - lo)], U8, name="w%d" % lo, align_bytes=64) for lo, hi in W_GROUPS]
        dx_sb = {1: keep.tile([P, TILES, 2 * C], BF16, name="dx_first"), 2: keep.tile([P, TILES, 2 * C], BF16, name="dx_mid")}
        u_codes = {job: keep.tile([P, P], U32, name="uc%d%d" % job, align_bytes=64) for job in JOBS}
        u_scales = {job: keep.tile([P, P], U8, name="us%d%d" % job, align_bytes=64) for job in JOBS}
        acc = {job: keep.tile([P, H], F32, name="acc%d%d" % job) for job in JOBS}
        out_codes = keep.tile([P, B], U32, align_bytes=64)
        out_scales = keep.tile([P, B], U8, align_bytes=64)

        def load_z(i):
            nc.sync.dma_start(out=z_sb[i][:], in_=z0[i * P : (i + 1) * P, :])

        def load_w(k):
            lo, hi = W_GROUPS[k]
            nc.sync.dma_start(out=w_sb[k][:].bitcast(I32), in_=w_words[0][:, 2 * H * lo : 2 * H * hi].bitcast(I32))

        def w_codes(c):
            k = [lo <= c < hi for lo, hi in W_GROUPS].index(True)
            first = 2 * H * (c - W_GROUPS[k][0])
            return w_sb[k][:, first : first + 2 * H].bitcast(FP4X4)

        nc.vector.memset(w_plane[:].bitcast(I32), 0)
        make_identity(nc, ident[:])
        nc.scalar.dma_start(out=gain[:], in_=g.rearrange("(p t) -> p t", t=4))
        load_z(0)
        load_w(0)
        for r in range(4):
            nc.sync.dma_start(out=w_plane[:].bitcast(I32)[r:P:32, :], in_=w_scales[0].bitcast(I32)[r:16:4, :])
        nc.sync.dma_start(out=dx_sb[1][:, :, :C], in_=dx0.rearrange("(i p) c -> p i c", p=P))
        load_z(1)
        load_w(1)
        load_w(2)
        load_z(2)
        load_z(3)
        nc.sync.dma_start(out=dx_sb[2][:, :, :C], in_=dxm.rearrange("(i p) c -> p i c", p=P))

        held = {}

        def turn_words(key, src):
            words = src.bitcast(F32)
            bank = tr_psum.tile([P, 2, P], F32, name="turned", tag="turned")
            for u in range(2):
                nc.tensor.transpose(bank[:, u, :], words[:, u : H // 2 : 2], ident[:])
            held[key] = bank

        def gain_z0(i):
            bank = held.pop(("z", i))
            grouped = stage.tile([P, H], BF16, name="grouped", tag="grouped", align_bytes=64)
            nc.vector.tensor_tensor(
                out=grouped[:].rearrange("p (b u e) -> p b u e", u=2, e=2),
                in0=bank[:].rearrange("p u b -> p (u b)").bitcast(BF16).rearrange("p (u b e) -> p b u e", u=2, e=2),
                in1=gain[:].rearrange("p (u e) -> p u e", e=2).unsqueeze(1).to_broadcast([P, P, 2, 2]),
                op=MULT,
            )
            held[("u", 1, i)] = grouped

        def gain_zmid(i):
            bank = held.pop(("zmid", i))
            grouped = stage.tile([P, H], BF16, name="grouped", tag="grouped", align_bytes=64)
            nc.vector.tensor_tensor(
                out=grouped[:].rearrange("p (b t) -> p b t", t=4),
                in0=bank[:].rearrange("p t b -> p b t"),
                in1=gain[:].unsqueeze(1).to_broadcast([P, P, 4]),
                op=MULT,
            )
            held[("u", 2, i)] = grouped

        def quantize_u(job):
            grouped = held.pop(("u",) + job)
            nc.vector.quantize_mx(out=u_codes[job][:].bitcast(FP8X4), scales=u_scales[job][:], in_=grouped[:])

        def add_turned(i, sources, first, last):
            if first:
                held[("zmid", i)] = tr_psum.tile([P, 4, P], F32, name="turned", tag="turned")
            bank = held[("zmid", i)]
            for s, src in enumerate(sources):
                for t in range(4):
                    nc.tensor.matmul(
                        bank[:, t, :],
                        lhsT=src[:, t * P : (t + 1) * P],
                        rhs=ident[:],
                        is_transpose=True,
                        start=(first and s == 0 and t == 0),
                        stop=(last and s == len(sources) - 1 and t == 3),
                    )

        def field_matmul(n):
            job, c = JOBS[n // C], n % C
            bank = mx_psum.tile([P, H], F32, name="field", tag="field")
            nc.tensor.matmul_mx(
                out=bank[:],
                lhsT=u_codes[job][:].bitcast(FP8X4),
                lhsT_scale=u_scales[job][:],
                rhs=w_codes(c),
                rhs_scale=w_plane[:, c * H : (c + 1) * H],
                start=True,
                stop=True,
            )
            held[("field", n)] = bank

        def tanh_and_weigh(n):
            job, c = JOBS[n // C], n % C
            step, i = job
            bank = held.pop(("field", n))
            f = flow.tile([P, H], F32, name="f", tag="f")
            dx = dx_sb[step][:, i, c : c + 1]
            total = acc[job]
            if step == 1:
                nc.scalar.activation(
                    out=f[:].rearrange("b (t p) -> b t p", t=4), in_=bank[:].rearrange("b (p t) -> b t p", t=4), func=TANH
                )
                if c % 2 == 0:
                    scaled = flow.tile([P, H], F32, name="scaled", tag="scaled")
                    nc.vector.tensor_scalar(out=scaled[:], in0=f[:], scalar1=dx, scalar2=None, op0=MULT)
                    held[("scaled", i, c)] = scaled
                elif c == 1:
                    nc.vector.scalar_tensor_tensor(
                        out=total[:].rearrange("b (t p) -> b t p", t=4),
                        in0=f[:].rearrange("b (t p) -> b t p", t=4),
                        scalar=dx,
                        in1=z_sb[i][:].rearrange("b (p t) -> b t p", t=4),
                        op0=MULT,
                        op1=ADD,
                    )
                else:
                    nc.vector.scalar_tensor_tensor(out=total[:], in0=f[:], scalar=dx, in1=total[:], op0=MULT, op1=ADD)
                return
            nc.scalar.activation(out=f[:], in_=bank[:], func=TANH)
            if c == 0:
                nc.vector.tensor_scalar(out=total[:], in0=f[:], scalar1=dx, scalar2=None, op0=MULT)
            else:
                for cols in (slice(0, HALF), slice(HALF, H)):
                    nc.vector.scalar_tensor_tensor(
                        out=total[:, cols], in0=f[:, cols], scalar=dx, in1=total[:, cols], op0=MULT, op1=ADD
                    )

        def store_out(i):
            nc.sync.dma_start(out=out_0[i * P : (i + 1) * P, :], in_=acc[(2, i)][:])

        def round_out(i):
            rounded = stage.tile([P, H], BF16, name="rounded", tag="rounded")
            nc.vector.tensor_copy(out=rounded[:], in_=acc[(2, i)][:])
            held[("rounded", i)] = rounded

        def group_out(i, on_scalar):
            bank = held.pop(("out", i))
            grouped = stage.tile([P, H], BF16, name="grouped", tag="grouped", align_bytes=64)
            dst = grouped[:].bitcast(F32).rearrange("p (b u) -> p b u", u=2)
            src = bank[:].rearrange("p u b -> p b u")
            if on_scalar:
                nc.scalar.copy(out=dst, in_=src)
            else:
                nc.vector.tensor_copy(out=dst, in_=src)
            held[("planes", i)] = grouped

        def quantize_out(i):
            grouped = held.pop(("planes", i))
            cols = slice(i * P, (i + 1) * P)
            nc.vector.quantize_mx(out=out_codes[:, cols].bitcast(FP8X4), scales=out_scales[:, cols], in_=grouped[:])
            nc.sync.dma_start(
                out=out_1[0].rearrange("p m t -> p (m t)").bitcast(I32)[:, cols], in_=out_codes[:, cols].bitcast(I32)
            )

        tensor_extra = {n: [] for n in range(UNITS)}
        vector_extra = {n: [] for n in range(UNITS)}
        for i, at in ((1, 0), (2, 2), (3, 11)):
            tensor_extra[at].append(lambda i=i: turn_words(("z", i), z_sb[i][:]))
            vector_extra[at + 1].append(lambda i=i: gain_z0(i))
            vector_extra[at + 2].append(lambda i=i: quantize_u((1, i)))
        for j, (step, i) in enumerate(JOBS):
            s = j * C
            if step == 1:
                tensor_extra[s + 5].append(
                    lambda i=i: add_turned(i, [held.pop(("scaled", i, c)) for c in (0, 2)], True, False)
                )
                tensor_extra[s + 9].append(
                    lambda i=i: add_turned(i, [held.pop(("scaled", i, c)) for c in (4, 6)] + [acc[(1, i)]], False, True)
                )
                vector_extra[s + 10].append(lambda i=i: gain_zmid(i))
                vector_extra[s + 11].append(lambda i=i: quantize_u((2, i)))
            elif i < TILES - 1:
                vector_extra[s + 7].append(lambda i=i: store_out(i))
                vector_extra[s + 8].append(lambda i=i: round_out(i))
                tensor_extra[s + 11].append(lambda i=i: turn_words(("out", i), held.pop(("rounded", i))[:]))
                if i < TILES - 2:
                    vector_extra[s + 12].append(lambda i=i: group_out(i, False))
                    vector_extra[s + 13].append(lambda i=i: quantize_out(i))

        turn_words(("z", 0), z_sb[0][:])
        gain_z0(0)
        quantize_u((1, 0))
        for n in range(AHEAD):
            field_matmul(n)
        for n in range(UNITS - 1):
            if n + AHEAD < UNITS:
                field_matmul(n + AHEAD)
            for job_part in tensor_extra[n]:
                job_part()
            tanh_and_weigh(n)
            for job_part in vector_extra[n]:
                job_part()

        last = TILES - 1
        bank = held.pop(("field", UNITS - 1))
        f = flow.tile([P, H], F32, name="f", tag="f")
        rounded = stage.tile([P, H], BF16, name="rounded", tag="rounded")
        total = acc[(2, last)]
        dx = dx_sb[2][:, last, C - 1 : C]
        for cols in (slice(0, HALF), slice(HALF, H)):
            nc.scalar.activation(out=f[:, cols], in_=bank[:, cols], func=TANH)
            nc.vector.scalar_tensor_tensor(
                out=rounded[:, cols], in0=f[:, cols], scalar=dx, in1=total[:, cols], op0=MULT, op1=ADD
            )
        group_out(last - 1, True)
        turn_words(("out", last), rounded[:])
        nc.vector.scalar_tensor_tensor(out=total[:], in0=f[:], scalar=dx, in1=total[:], op0=MULT, op1=ADD)
        store_out(last)
        quantize_out(last - 1)
        group_out(last, True)
        quantize_out(last)
        for r in range(4):
            queue = nc.sync if r < 2 else nc.scalar
            queue.dma_start(out=out_2[0].bitcast(I32)[r:16:4, :], in_=out_scales[:].bitcast(I32)[r:P:32, :])
